import numpy as np
import ml_dtypes


def mxq(x, axis, fmt="e4m3"):
    dtype, down = {"e4m3": (ml_dtypes.float8_e4m3fn, 7), "e5m2": (ml_dtypes.float8_e5m2, 14)}[fmt]
    v = np.moveaxis(np.asarray(x, np.float32).astype(ml_dtypes.bfloat16).astype(np.float64), axis, -1)
    blocks = v.reshape(v.shape[:-1] + (-1, 32))
    amax = np.abs(blocks).max(-1, keepdims=True)
    byte = np.maximum(np.where(amax > 0, np.frexp(amax)[1] - 1 + 127, 0) - down, 1)
    scale = np.exp2(byte - 127.0)
    codes = (blocks / scale).astype(np.float32).astype(dtype).astype(np.float64)
    return np.moveaxis((codes * scale).reshape(v.shape), -1, axis)


WIDE = False


def mx_kscale(k):
    if not WIDE:
        return np.ones(k)
    levels = np.array([10, -10, 5, -5, 0])
    if k % 512:
        return np.exp2(np.random.permutation(np.resize(levels, k // 32))).repeat(32)
    a = np.empty((k // 512, 16))
    for p in range(k // 512):
        a[p, :8] = np.random.permutation(np.resize(levels, 8))
        for g in range(8):
            far = levels[np.abs(levels - a[p, g]) >= 10]
            a[p, g + 8] = far[np.random.randint(len(far))]
    return np.exp2(a.ravel()).repeat(32)


def f64(x):
    return np.asarray(x).astype(np.float64)


def striped(idx):
    return np.tile(idx.reshape(-1, 16).T, (8, 1)).astype(np.uint16)


def unstriped(offs):
    return offs[:16].T.reshape(-1).astype(np.int64)


def striped8(idx):
    return np.concatenate([x.reshape(-1, 16).T for x in idx]).astype(np.uint16)


def runs(offs, k):
    lists = np.stack([offs[16 * r : 16 * r + 16].T.reshape(-1) for r in range(8)]).astype(np.int64)
    return lists[np.arange(k) % 512 // 64]


def pack_weight(w):
    k, n = w.shape
    w = f64(np.asarray(w, np.float32).astype(ml_dtypes.bfloat16)).reshape(k // 32, 32, n)
    amax = np.abs(w).max(1)
    byte = np.clip(np.where(amax > 0, np.frexp(amax)[1] - 1 + 127 - 7, 1), 1, 254)
    scaled = (w * np.exp2(127.0 - byte)[:, None, :]).reshape(k, n).astype(np.float32)
    words = np.ascontiguousarray(scaled.reshape(k // 512, 128, 4, n).transpose(0, 1, 3, 2)).astype(ml_dtypes.float8_e4m3fn).view(np.uint8)
    return words, np.ascontiguousarray(byte.astype(np.uint8).reshape(k // 512, 16, n))


def unpack_weight(words, scales):
    g, p, n, _ = words.shape
    vals = np.ascontiguousarray(words).view(ml_dtypes.float8_e4m3fn).astype(np.float64) * np.repeat(np.exp2(scales.astype(np.float64) - 127.0), 8, axis=1)[..., None]
    return vals.transpose(0, 1, 3, 2).reshape(g * 512, n)


K, T, S, N, H = 512, 2048, 512, 512, 512


def setup_inputs():
    n = np.random.standard_normal
    s = mx_kscale(K)[:, None]
    u = mx_kscale(H)
    packed_xT = pack_weight(n((K, T)) * s)
    return {
        "x_words": packed_xT[0],
        "x_scales": packed_xT[1],
        "w1": (n((K, H)) / np.sqrt(K) / s).astype(np.float32),
        "gn": (np.random.uniform(0.5, 1.5, (H, 1)) * u[:, None]).astype(np.float32),
        "gm": (np.random.uniform(0.5, 1.5, (H, 1)) * u[:, None]).astype(np.float32),
        "w2": (n((H, N)) / np.sqrt(2 * H) / u[:, None]).astype(np.float32),
        "w3": (n((H, N)) / np.sqrt(2 * H) / u[:, None]).astype(np.float32),
        "offs": striped(np.random.permutation(T)[:S]),
        "n1": striped8(np.stack([np.random.permutation(S) for _ in range(8)])),
        "n2": striped8(np.stack([np.random.permutation(S) for _ in range(8)])),
        "n3": striped8(np.stack([np.random.permutation(S) for _ in range(8)])),
        "n4": striped8(np.stack([np.random.permutation(S) for _ in range(8)])),
        "n5": striped8(np.stack([np.random.permutation(S) for _ in range(8)])),
    }


def reference(x_words, x_scales, w1, gn, gm, w2, w3, offs, n1, n2, n3, n4, n5):
    xq = unpack_weight(x_words, x_scales)[:, unstriped(offs)]
    y = mxq(f64(w1), 0, "e4m3").T @ xq
    st = y + y[np.arange(H)[:, None], runs(n1, H)]
    z = f64(gn) * (st * (np.tanh(st[np.arange(H)[:, None], runs(n2, H)])))
    pa = y[np.arange(H)[:, None], runs(n3, H)]
    z2 = f64(gm) * ((2.0 * (y * pa)) / ((y) ** 2 + (pa) ** 2 + 0.5))
    h = mxq(f64(w2), 0, "e4m3").T @ mxq(z, 0, "e4m3") + mxq(f64(w3), 0, "e4m3").T @ mxq(z2, 0, "e4m3")
    return h - (np.minimum(h[np.arange(N)[:, None], runs(n4, N)], h[np.arange(N)[:, None], runs(n5, N)]))

@@ -1,0 +1,237 @@
+from contextlib import ExitStack
+
+import concourse.mybir as mybir
+from concourse.masks import make_identity
+
+K, T, S, N, H = 512, 2048, 512, 512, 512
+FLOPS = 2 * K * H * S + 2 * 2 * H * N * S
+
+F32 = mybir.dt.float32
+BF16 = mybir.dt.bfloat16
+I32 = mybir.dt.int32
+U32 = mybir.dt.uint32
+U16 = mybir.dt.uint16
+U8 = mybir.dt.uint8
+FP8X4 = mybir.dt.float8_e4m3fn_x4
+ALU = mybir.AluOpType
+ACT = mybir.ActivationFunctionType
+
+P = 128
+PACK = 4
+HALF = S // 2
+LIST_COLS = S // 16
+
+
+def tile_picked_joinhoppharmunder_none_p_kernel(
+    tc, x_words, x_scales, w1, gn, gm, w2, w3, offs, n1, n2, n3, n4, n5, out
+):
+    nc = tc.nc
+    with ExitStack() as ctx:
+        keep = ctx.enter_context(tc.tile_pool(name="keep", bufs=1))
+        psum = ctx.enter_context(tc.psum_pool(name="psum", bufs=1))
+
+        def planes(name):
+            return [keep.tile([P, S], F32, name=f"{name}{t}", align_bytes=64) for t in range(PACK)]
+
+        def load_list(name, src):
+            tile = keep.tile([P, LIST_COLS], U16, name=name)
+            nc.sync.dma_start(tile[:], src)
+            return tile
+
+        def load_weight(name, src):
+            tile = keep.tile([P, PACK, 512], F32, name=name, align_bytes=64)
+            nc.sync.dma_start(tile[:], src.rearrange("(p j) c -> p j c", j=PACK))
+            return tile
+
+        def load_gain(name, src):
+            tile = keep.tile([P, PACK], F32, name=name)
+            nc.sync.dma_start(tile[:], src.rearrange("(p t) o -> p (t o)", t=PACK))
+            return tile
+
+        def cols(half):
+            return slice(half * HALF, (half + 1) * HALF)
+
+        def entries(lst, half):
+            return lst[:, half * LIST_COLS // 2 : (half + 1) * LIST_COLS // 2]
+
+        def deal_views(name, raw):
+            grouped = keep.tile([P, 4 * 512], BF16, name=name, align_bytes=64)
+            dst = grouped[:].rearrange("p (t m j) -> p m j t", t=PACK, j=PACK)
+            src = raw[:].rearrange("p j (m t) -> p m j t", t=PACK)
+            return grouped, dst, src
+
+        def mx_tiles(name):
+            codes = keep.tile([P, 512], U32, name=name + "_codes", align_bytes=64)
+            scales = keep.tile([P, 512], U8, name=name + "_scales", align_bytes=64)
+            return codes, scales
+
+        def quantize(mx, grouped, first, count):
+            nc.vector.quantize_mx(
+                out=mx[0][:, first : first + count].bitcast(FP8X4),
+                scales=mx[1][:, first : first + count],
+                in_=grouped[:, PACK * first : PACK * (first + count)],
+            )
+
+        def product(acc, lhs, t, rhs, half, start, stop):
+            m_cols = slice(t * P, (t + 1) * P)
+            nc.tensor.matmul_mx(
+                out=acc[:, cols(half)],
+                lhsT=lhs[0][:, m_cols].bitcast(FP8X4),
+                lhsT_scale=lhs[1][:, m_cols],
+                rhs=rhs[0][:, cols(half)].bitcast(FP8X4),
+                rhs_scale=rhs[1][:, cols(half)],
+                start=start,
+                stop=stop,
+            )
+
+        xs_table = keep.tile([P, T], U8, name="xs_table", align_bytes=64)
+        xs_rows = keep.tile([P, T], U8, name="xs_rows", align_bytes=64)
+        for q in range(4):
+            nc.scalar.dma_start(
+                xs_rows[32 * q : 32 * q + 4, :].bitcast(I32), x_scales[0, 4 * q : 4 * q + 4, :].bitcast(I32)
+            )
+        nc.vector.memset(xs_table[:].bitcast(I32), 0)
+        offs_sb = load_list("offs_sb", offs)
+        w1_raw = load_weight("w1_raw", w1)
+        xw_table = keep.tile([P, T], U32, name="xw_table", align_bytes=64)
+        nc.sync.dma_start(xw_table[:].bitcast(I32), x_words[0].rearrange("p n t -> p (n t)").bitcast(I32))
+        n3_sb = load_list("n3_sb", n3)
+        gm_sb = load_gain("gm_sb", gm)
+        n1_sb = load_list("n1_sb", n1)
+        w2_raw = load_weight("w2_raw", w2)
+        w3_raw = load_weight("w3_raw", w3)
+        gn_sb = load_gain("gn_sb", gn)
+        n2_sb = load_list("n2_sb", n2)
+        n4_sb = load_list("n4_sb", n4)
+        n5_sb = load_list("n5_sb", n5)
+
+        quarter = keep.tile([P, 1], F32, name="quarter")
+        nc.gpsimd.memset(quarter[:], 0.25)
+        warm = keep.tile([P, 1], F32, name="warm")
+        nc.scalar.activation(warm[:], quarter[:], ACT.Ln)
+        ident = keep.tile([P, P], F32, name="ident", align_bytes=64)
+        make_identity(nc, ident[:])
+
+        xq = mx_tiles("xq")
+        for q in range(4):
+            rows = slice(32 * q, 32 * q + 4)
+            nc.vector.tensor_copy(xs_table[rows, :].bitcast(I32), xs_rows[rows, :].bitcast(I32))
+        nc.vector.tensor_copy(xq[1][:], xs_table[:].indirect(offs_sb[:]))
+        w1_bf, dst, src = deal_views("w1_bf", w1_raw)
+        nc.scalar.copy(dst[:, : P // 2], src[:, : P // 2])
+        nc.vector.tensor_copy(dst[:, P // 2 :], src[:, P // 2 :])
+        w1q = mx_tiles("w1q")
+        quantize(w1q, w1_bf, 0, 512)
+        y_ps = [psum.tile([P, S], F32, name=f"y_ps{t}", tag=f"bank_a{t}") for t in range(PACK)]
+        y = planes("y")
+        for half in range(2):
+            nc.vector.tensor_copy(xq[0][:, cols(half)], xw_table[:].indirect(entries(offs_sb, half)))
+            for t in range(PACK):
+                product(y_ps[t], w1q, t, xq, half, True, True)
+                nc.scalar.copy(y[t][:, cols(half)], y_ps[t][:, cols(half)])
+
+        y_copy = planes("y_copy")
+        for t in range(PACK):
+            nc.sync.dma_start(y_copy[t][:], y[t][:])
+
+        pa, y_sq, pa_sq, st, st_gain, tanh_st = (planes(s) for s in ("pa", "y_sq", "pa_sq", "st", "st_gain", "tanh_st"))
+        num = keep.tile([P, PACK, S], F32, name="num", align_bytes=64)
+        log_den = keep.tile([P, PACK, S], F32, name="log_den", align_bytes=64)
+        recip_t = keep.tile([P, PACK, S], F32, name="recip_t", align_bytes=64)
+
+        def numerator(t):
+            nc.vector.scalar_tensor_tensor(
+                num[:, t, :], pa[t][:], gm_sb[:, t : t + 1], y_ps[t][:], ALU.mult, ALU.mult
+            )
+
+        for t in range(PACK):
+            nc.scalar.activation(y_sq[t][:], y[t][:], ACT.Square)
+        for t in range(PACK):
+            for half in range(2):
+                nc.vector.tensor_copy(pa[t][:, cols(half)], y[t][:].indirect(entries(n3_sb, half)))
+            if t > 0:
+                numerator(t - 1)
+            nc.scalar.activation(pa_sq[t][:], pa[t][:], ACT.Square)
+            den_ps = psum.tile([P, S], F32, name=f"den_ps{t}", tag=f"bank_b{t}")
+            for b in range(4):
+                blk = slice(b * P, (b + 1) * P)
+                nc.tensor.matmul(den_ps[:, blk], y_sq[t][:, blk], ident[:], start=True, stop=False, is_transpose=True)
+                nc.tensor.matmul(den_ps[:, blk], pa_sq[t][:, blk], ident[:], start=False, stop=True, is_transpose=True)
+            nc.scalar.activation(log_den[:, t, :], den_ps[:], ACT.Ln, bias=quarter[:], scale=0.5)
+
+        for t in range(PACK):
+            for half in range(2):
+                nc.vector.tensor_tensor(
+                    st[t][:, cols(half)], y[t][:].indirect(entries(n1_sb, half)), y_copy[t][:, cols(half)], ALU.add
+                )
+            if t == 0:
+                numerator(PACK - 1)
+            else:
+                nc.vector.tensor_scalar(st_gain[t - 1][:], st[t - 1][:], gn_sb[:, t - 1 : t], None, ALU.mult)
+            nc.scalar.activation(tanh_st[t][:], st[t][:], ACT.Tanh)
+
+        nc.scalar.activation(recip_t[:], log_den[:], ACT.Exp, scale=-1.0)
+        r_ps = [psum.tile([P, PACK, P], F32, name=f"r_ps{b}", tag=f"bank_b{b}") for b in range(4)]
+        for b in range(4):
+            for t in range(PACK):
+                nc.tensor.transpose(r_ps[b][:, t, :], recip_t[:, t, b * P : (b + 1) * P], ident[:])
+
+        w2_bf, dst, src = deal_views("w2_bf", w2_raw)
+        nc.scalar.copy(dst, src)
+        w3_bf, dst, src = deal_views("w3_bf", w3_raw)
+        nc.scalar.copy(dst, src)
+
+        z = keep.tile([P, PACK, S], F32, name="z", align_bytes=64)
+        z_bf = keep.tile([P, PACK * S], BF16, name="z_bf", align_bytes=64)
+        z2_bf = keep.tile([P, PACK * S], BF16, name="z2_bf", align_bytes=64)
+        for half in range(2):
+            for t in range(PACK):
+                nc.vector.tensor_tensor(
+                    z[:, t, cols(half)], tanh_st[t][:].indirect(entries(n2_sb, half)), st_gain[t][:, cols(half)], ALU.mult
+                )
+                if half == 0 and t == 0:
+                    nc.vector.tensor_scalar(st_gain[3][:], st[3][:], gn_sb[:, 3:4], None, ALU.mult)
+            nc.scalar.copy(
+                z_bf[:, half * PACK * HALF : (half + 1) * PACK * HALF].rearrange("p (c i t) -> p c t i", i=4, t=PACK),
+                z[:, :, cols(half)].rearrange("p t (c i) -> p c t i", i=4),
+            )
+
+        w2q, w3q, zq, z2q = (mx_tiles(s) for s in ("w2q", "w3q", "zq", "z2q"))
+        for b in range(4):
+            nc.vector.tensor_tensor(
+                z2_bf[:, b * PACK * P : (b + 1) * PACK * P].rearrange("p (c i t) -> p c t i", i=4, t=PACK),
+                num[:, :, b * P : (b + 1) * P].rearrange("p t (c i) -> p c t i", i=4),
+                r_ps[b][:].rearrange("p t (c i) -> p c t i", i=4),
+                ALU.mult,
+            )
+        quantize(w2q, w2_bf, 0, 512)
+        quantize(w3q, w3_bf, 0, 512)
+
+        h_ps = [psum.tile([P, S], F32, name=f"h_ps{t}", tag=f"bank_a{t}") for t in range(PACK)]
+        h, neg_h, e4, e5, res = (planes(s) for s in ("h", "neg_h", "e4", "e5", "res"))
+        for half in range(2):
+            quantize(z2q, z2_bf, half * HALF, HALF)
+            quantize(zq, z_bf, half * HALF, HALF)
+            for t in range(PACK):
+                product(h_ps[t], w3q, t, z2q, half, True, False)
+                product(h_ps[t], w2q, t, zq, half, False, True)
+                nc.scalar.mul(neg_h[t][:, cols(half)], h_ps[t][:, cols(half)], -1.0)
+                nc.scalar.copy(h[t][:, cols(half)], h_ps[t][:, cols(half)])
+
+        out_rows = out.rearrange("(p t) j -> p t j", t=PACK)
+        steps = [(t, half) for t in range(PACK) for half in range(2)]
+
+        def finish(t, half):
+            nc.vector.tensor_tensor(res[t][:, cols(half)], e4[t][:, cols(half)], e5[t][:, cols(half)], ALU.max)
+            nc.sync.dma_start(out_rows[:, t, cols(half)], res[t][:, cols(half)])
+
+        for i, (t, half) in enumerate(steps):
+            nc.vector.tensor_tensor(
+                e4[t][:, cols(half)], neg_h[t][:].indirect(entries(n4_sb, half)), h[t][:, cols(half)], ALU.add
+            )
+            if i > 0:
+                finish(*steps[i - 1])
+            nc.vector.tensor_tensor(
+                e5[t][:, cols(half)], neg_h[t][:].indirect(entries(n5_sb, half)), h[t][:, cols(half)], ALU.add
+            )
+        finish(*steps[-1])

@@ -28,10 +28,11 @@ def tile_picked_joinhoppharmunder_none_p_kernel(
     nc = tc.nc
     with ExitStack() as ctx:
         keep = ctx.enter_context(tc.tile_pool(name="keep", bufs=1))
+        shared = ctx.enter_context(tc.tile_pool(name="shared", bufs=1))
         psum = ctx.enter_context(tc.psum_pool(name="psum", bufs=1))
 
-        def planes(name):
-            return [keep.tile([P, S], F32, name=f"{name}{t}", align_bytes=64) for t in range(PACK)]
+        def planes(name, width=S):
+            return [keep.tile([P, width], F32, name=f"{name}{t}", align_bytes=64) for t in range(PACK)]
 
         def load_list(name, src):
             tile = keep.tile([P, LIST_COLS], U16, name=name)
@@ -54,10 +55,10 @@ def tile_picked_joinhoppharmunder_none_p_kernel(
         def entries(lst, half):
             return lst[:, half * LIST_COLS // 2 : (half + 1) * LIST_COLS // 2]
 
-        def deal_views(name, raw):
+        def deal_views(name, raw, order):
             grouped = keep.tile([P, 4 * 512], BF16, name=name, align_bytes=64)
-            dst = grouped[:].rearrange("p (t m j) -> p m j t", t=PACK, j=PACK)
-            src = raw[:].rearrange("p j (m t) -> p m j t", t=PACK)
+            dst = grouped[:].rearrange("p (t m j) -> " + order, t=PACK, j=PACK)
+            src = raw[:].rearrange("p j (m t) -> " + order, t=PACK)
             return grouped, dst, src
 
         def mx_tiles(name):
@@ -87,12 +88,12 @@ def tile_picked_joinhoppharmunder_none_p_kernel(
         xs_table = keep.tile([P, T], U8, name="xs_table", align_bytes=64)
         xs_rows = keep.tile([P, T], U8, name="xs_rows", align_bytes=64)
         for q in range(4):
-            nc.scalar.dma_start(
+            nc.sync.dma_start(
                 xs_rows[32 * q : 32 * q + 4, :].bitcast(I32), x_scales[0, 4 * q : 4 * q + 4, :].bitcast(I32)
             )
         nc.vector.memset(xs_table[:].bitcast(I32), 0)
-        offs_sb = load_list("offs_sb", offs)
         w1_raw = load_weight("w1_raw", w1)
+        offs_sb = load_list("offs_sb", offs)
         xw_table = keep.tile([P, T], U32, name="xw_table", align_bytes=64)
         nc.sync.dma_start(xw_table[:].bitcast(I32), x_words[0].rearrange("p n t -> p (n t)").bitcast(I32))
         n3_sb = load_list("n3_sb", n3)
@@ -117,13 +118,14 @@ def tile_picked_joinhoppharmunder_none_p_kernel(
             rows = slice(32 * q, 32 * q + 4)
             nc.vector.tensor_copy(xs_table[rows, :].bitcast(I32), xs_rows[rows, :].bitcast(I32))
         nc.vector.tensor_copy(xq[1][:], xs_table[:].indirect(offs_sb[:]))
-        w1_bf, dst, src = deal_views("w1_bf", w1_raw)
+        w1_bf, dst, src = deal_views("w1_bf", w1_raw, "p m j t")
         nc.scalar.copy(dst[:, : P // 2], src[:, : P // 2])
         nc.vector.tensor_copy(dst[:, P // 2 :], src[:, P // 2 :])
         w1q = mx_tiles("w1q")
-        quantize(w1q, w1_bf, 0, 512)
+        for t in range(PACK):
+            quantize(w1q, w1_bf, t * P, P)
         y_ps = [psum.tile([P, S], F32, name=f"y_ps{t}", tag=f"bank_a{t}") for t in range(PACK)]
-        y = planes("y")
+        y = planes("y", 2 * S)
         for half in range(2):
             nc.vector.tensor_copy(xq[0][:, cols(half)], xw_table[:].indirect(entries(offs_sb, half)))
             for t in range(PACK):
@@ -132,9 +134,16 @@ def tile_picked_joinhoppharmunder_none_p_kernel(
 
         y_copy = planes("y_copy")
         for t in range(PACK):
-            nc.sync.dma_start(y_copy[t][:], y[t][:])
+            nc.sync.dma_start(y_copy[t][:], y[t][:, :S])
 
-        pa, y_sq, pa_sq, st, st_gain, tanh_st = (planes(s) for s in ("pa", "y_sq", "pa_sq", "st", "st_gain", "tanh_st"))
+        w2_bf, dst, src = deal_views("w2_bf", w2_raw, "p m t j")
+        nc.gpsimd.tensor_scalar(dst, src, 1.0, 0.0, ALU.mult, ALU.add)
+        w3_bf, dst, src = deal_views("w3_bf", w3_raw, "p m t j")
+        nc.gpsimd.tensor_scalar(dst, src, 1.0, 0.0, ALU.mult, ALU.add)
+
+        pa, y_sq, st, st_gain = (planes(s) for s in ("pa", "y_sq", "st", "st_gain"))
+        pa_sq = shared.tile([P, PACK, S], F32, name="pa_sq", offset=0)
+        tanh_st = [shared.tile([P, S], F32, name=f"tanh_st{t}", offset=t * S * 4) for t in range(PACK)]
         num = keep.tile([P, PACK, S], F32, name="num", align_bytes=64)
         log_den = keep.tile([P, PACK, S], F32, name="log_den", align_bytes=64)
         recip_t = keep.tile([P, PACK, S], F32, name="recip_t", align_bytes=64)
@@ -145,41 +154,34 @@ def tile_picked_joinhoppharmunder_none_p_kernel(
             )
 
         for t in range(PACK):
-            nc.scalar.activation(y_sq[t][:], y[t][:], ACT.Square)
+            nc.scalar.activation(y_sq[t][:], y[t][:, :S], ACT.Square)
         for t in range(PACK):
-            for half in range(2):
-                nc.vector.tensor_copy(pa[t][:, cols(half)], y[t][:].indirect(entries(n3_sb, half)))
+            nc.vector.tensor_copy(pa[t][:], y[t][:].indirect(n3_sb[:]))
             if t > 0:
                 numerator(t - 1)
-            nc.scalar.activation(pa_sq[t][:], pa[t][:], ACT.Square)
+            nc.scalar.activation(pa_sq[:, t, :], pa[t][:], ACT.Square)
             den_ps = psum.tile([P, S], F32, name=f"den_ps{t}", tag=f"bank_b{t}")
             for b in range(4):
                 blk = slice(b * P, (b + 1) * P)
                 nc.tensor.matmul(den_ps[:, blk], y_sq[t][:, blk], ident[:], start=True, stop=False, is_transpose=True)
-                nc.tensor.matmul(den_ps[:, blk], pa_sq[t][:, blk], ident[:], start=False, stop=True, is_transpose=True)
+                nc.tensor.matmul(den_ps[:, blk], pa_sq[:, t, blk], ident[:], start=False, stop=True, is_transpose=True)
             nc.scalar.activation(log_den[:, t, :], den_ps[:], ACT.Ln, bias=quarter[:], scale=0.5)
 
         for t in range(PACK):
-            for half in range(2):
-                nc.vector.tensor_tensor(
-                    st[t][:, cols(half)], y[t][:].indirect(entries(n1_sb, half)), y_copy[t][:, cols(half)], ALU.add
-                )
+            nc.vector.tensor_tensor(st[t][:], y[t][:].indirect(n1_sb[:]), y_copy[t][:], ALU.add)
             if t == 0:
                 numerator(PACK - 1)
             else:
                 nc.vector.tensor_scalar(st_gain[t - 1][:], st[t - 1][:], gn_sb[:, t - 1 : t], None, ALU.mult)
             nc.scalar.activation(tanh_st[t][:], st[t][:], ACT.Tanh)
 
-        nc.scalar.activation(recip_t[:], log_den[:], ACT.Exp, scale=-1.0)
         r_ps = [psum.tile([P, PACK, P], F32, name=f"r_ps{b}", tag=f"bank_b{b}") for b in range(4)]
         for b in range(4):
+            blk = slice(b * P, (b + 1) * P)
+            nc.scalar.activation(recip_t[:, :, blk], log_den[:, :, blk], ACT.Exp, scale=-1.0)
             for t in range(PACK):
                 nc.tensor.transpose(r_ps[b][:, t, :], recip_t[:, t, b * P : (b + 1) * P], ident[:])
 
-        w2_bf, dst, src = deal_views("w2_bf", w2_raw)
-        nc.scalar.copy(dst, src)
-        w3_bf, dst, src = deal_views("w3_bf", w3_raw)
-        nc.scalar.copy(dst, src)
 
         z = keep.tile([P, PACK, S], F32, name="z", align_bytes=64)
         z_bf = keep.tile([P, PACK * S], BF16, name="z_bf", align_bytes=64)
@@ -204,34 +206,39 @@ def tile_picked_joinhoppharmunder_none_p_kernel(
                 r_ps[b][:].rearrange("p t (c i) -> p c t i", i=4),
                 ALU.mult,
             )
-        quantize(w2q, w2_bf, 0, 512)
-        quantize(w3q, w3_bf, 0, 512)
+        quantize(w2q, w2_bf, 0, P)
+        quantize(w3q, w3_bf, 0, P)
 
         h_ps = [psum.tile([P, S], F32, name=f"h_ps{t}", tag=f"bank_a{t}") for t in range(PACK)]
-        h, neg_h, e4, e5, res = (planes(s) for s in ("h", "neg_h", "e4", "e5", "res"))
+        h, e4, e5, res = (planes(s) for s in ("h", "e4", "e5", "res"))
+        neg_h = planes("neg_h", 2 * S)
         for half in range(2):
             quantize(z2q, z2_bf, half * HALF, HALF)
             quantize(zq, z_bf, half * HALF, HALF)
-            for t in range(PACK):
+        for t in range(1, PACK):
+            quantize(w2q, w2_bf, t * P, P)
+            quantize(w3q, w3_bf, t * P, P)
+        for t in range(PACK):
+            for half in range(2):
                 product(h_ps[t], w3q, t, z2q, half, True, False)
                 product(h_ps[t], w2q, t, zq, half, False, True)
                 nc.scalar.mul(neg_h[t][:, cols(half)], h_ps[t][:, cols(half)], -1.0)
                 nc.scalar.copy(h[t][:, cols(half)], h_ps[t][:, cols(half)])
 
         out_rows = out.rearrange("(p t) j -> p t j", t=PACK)
-        steps = [(t, half) for t in range(PACK) for half in range(2)]
+        steps = [(t, 0, S) for t in range(PACK - 1)] + [(PACK - 1, 0, HALF), (PACK - 1, HALF, S)]
 
-        def finish(t, half):
-            nc.vector.tensor_tensor(res[t][:, cols(half)], e4[t][:, cols(half)], e5[t][:, cols(half)], ALU.max)
-            nc.sync.dma_start(out_rows[:, t, cols(half)], res[t][:, cols(half)])
+        def finish(t, lo, hi):
+            nc.vector.tensor_tensor(res[t][:, lo:hi], e4[t][:, lo:hi], e5[t][:, lo:hi], ALU.max)
+            nc.sync.dma_start(out_rows[:, t, lo:hi], res[t][:, lo:hi])
 
-        for i, (t, half) in enumerate(steps):
+        for i, (t, lo, hi) in enumerate(steps):
             nc.vector.tensor_tensor(
-                e4[t][:, cols(half)], neg_h[t][:].indirect(entries(n4_sb, half)), h[t][:, cols(half)], ALU.add
+                e4[t][:, lo:hi], neg_h[t][:].indirect(n4_sb[:, lo // 16 : hi // 16]), h[t][:, lo:hi], ALU.add
             )
             if i > 0:
                 finish(*steps[i - 1])
             nc.vector.tensor_tensor(
-                e5[t][:, cols(half)], neg_h[t][:].indirect(entries(n5_sb, half)), h[t][:, cols(half)], ALU.add
+                e5[t][:, lo:hi], neg_h[t][:].indirect(n5_sb[:, lo // 16 : hi // 16]), h[t][:, lo:hi], ALU.add
             )
         finish(*steps[-1])

@@ -66,21 +66,21 @@ def tile_picked_joinhoppharmunder_none_p_kernel(
             scales = keep.tile([P, 512], U8, name=name + "_scales", align_bytes=64)
             return codes, scales
 
+        def mx_cols(mx, first, count):
+            return mx[0][:, first : first + count], mx[1][:, first : first + count]
+
         def quantize(mx, grouped, first, count):
             nc.vector.quantize_mx(
-                out=mx[0][:, first : first + count].bitcast(FP8X4),
-                scales=mx[1][:, first : first + count],
-                in_=grouped[:, PACK * first : PACK * (first + count)],
+                out=mx[0].bitcast(FP8X4), scales=mx[1], in_=grouped[:, PACK * first : PACK * (first + count)]
             )
 
-        def product(acc, lhs, t, rhs, half, start, stop):
-            m_cols = slice(t * P, (t + 1) * P)
+        def product(acc, lhs, rhs, start, stop):
             nc.tensor.matmul_mx(
-                out=acc[:, cols(half)],
-                lhsT=lhs[0][:, m_cols].bitcast(FP8X4),
-                lhsT_scale=lhs[1][:, m_cols],
-                rhs=rhs[0][:, cols(half)].bitcast(FP8X4),
-                rhs_scale=rhs[1][:, cols(half)],
+                out=acc,
+                lhsT=lhs[0].bitcast(FP8X4),
+                lhsT_scale=lhs[1],
+                rhs=rhs[0].bitcast(FP8X4),
+                rhs_scale=rhs[1],
                 start=start,
                 stop=stop,
             )
@@ -118,62 +118,68 @@ def tile_picked_joinhoppharmunder_none_p_kernel(
             rows = slice(32 * q, 32 * q + 4)
             nc.vector.tensor_copy(xs_table[rows, :].bitcast(I32), xs_rows[rows, :].bitcast(I32))
         nc.vector.tensor_copy(xq[1][:], xs_table[:].indirect(offs_sb[:]))
-        w1_bf, dst, src = deal_views("w1_bf", w1_raw, "p m j t")
+        w1_bf, dst, src = deal_views("w1_bf", w1_raw, "p m t j")
         nc.scalar.copy(dst[:, : P // 2], src[:, : P // 2])
         nc.vector.tensor_copy(dst[:, P // 2 :], src[:, P // 2 :])
         w1q = mx_tiles("w1q")
         for t in range(PACK):
-            quantize(w1q, w1_bf, t * P, P)
+            quantize(mx_cols(w1q, t * P, P), w1_bf, t * P, P)
         y_ps = [psum.tile([P, S], F32, name=f"y_ps{t}", tag=f"bank_a{t}") for t in range(PACK)]
         y = planes("y", 2 * S)
         for half in range(2):
             nc.vector.tensor_copy(xq[0][:, cols(half)], xw_table[:].indirect(entries(offs_sb, half)))
-            for t in range(PACK):
-                product(y_ps[t], w1q, t, xq, half, True, True)
-                nc.scalar.copy(y[t][:, cols(half)], y_ps[t][:, cols(half)])
+        for t, lo, hi in [(0, 0, HALF), (0, HALF, S), (1, 0, S), (2, 0, S), (3, 0, S)]:
+            product(y_ps[t][:, lo:hi], mx_cols(w1q, t * P, P), mx_cols(xq, lo, hi - lo), True, True)
+            nc.scalar.copy(y[t][:, lo:hi], y_ps[t][:, lo:hi])
 
-        y_copy = planes("y_copy")
+        y_copy = shared.tile([P, PACK, S], F32, name="y_copy", offset=16384, align_bytes=64)
         for t in range(PACK):
-            nc.sync.dma_start(y_copy[t][:], y[t][:, :S])
+            nc.sync.dma_start(y_copy[:, t, :], y[t][:, :S])
 
         w2_bf, dst, src = deal_views("w2_bf", w2_raw, "p m t j")
         nc.gpsimd.tensor_scalar(dst, src, 1.0, 0.0, ALU.mult, ALU.add)
         w3_bf, dst, src = deal_views("w3_bf", w3_raw, "p m t j")
         nc.gpsimd.tensor_scalar(dst, src, 1.0, 0.0, ALU.mult, ALU.add)
 
-        pa, y_sq, st, st_gain = (planes(s) for s in ("pa", "y_sq", "st", "st_gain"))
-        pa_sq = shared.tile([P, PACK, S], F32, name="pa_sq", offset=0)
-        tanh_st = [shared.tile([P, S], F32, name=f"tanh_st{t}", offset=t * S * 4) for t in range(PACK)]
+        pa = planes("pa")
+        st = [shared.tile([P, S], F32, name=f"st{t}", offset=32768 + t * S * 4, align_bytes=64) for t in range(PACK)]
+        st_gain = planes("st_gain")
+        squares = shared.tile([P, 2, PACK, S], F32, name="squares", offset=0, align_bytes=64)
+        tanh_st = [shared.tile([P, 2 * S], F32, name=f"tanh_st{t}", offset=t * S * 8, align_bytes=64) for t in range(PACK)]
         num = keep.tile([P, PACK, S], F32, name="num", align_bytes=64)
         log_den = keep.tile([P, PACK, S], F32, name="log_den", align_bytes=64)
-        recip_t = keep.tile([P, PACK, S], F32, name="recip_t", align_bytes=64)
+        recip_t = shared.tile([P, PACK, S], F32, name="recip_t", offset=32768, align_bytes=64)
 
         def numerator(t):
             nc.vector.scalar_tensor_tensor(
                 num[:, t, :], pa[t][:], gm_sb[:, t : t + 1], y_ps[t][:], ALU.mult, ALU.mult
             )
 
-        for t in range(PACK):
-            nc.scalar.activation(y_sq[t][:], y[t][:, :S], ACT.Square)
-        for t in range(PACK):
-            nc.vector.tensor_copy(pa[t][:], y[t][:].indirect(n3_sb[:]))
-            if t > 0:
-                numerator(t - 1)
-            nc.scalar.activation(pa_sq[:, t, :], pa[t][:], ACT.Square)
-            den_ps = psum.tile([P, S], F32, name=f"den_ps{t}", tag=f"bank_b{t}")
+        den_ps = [psum.tile([P, S], F32, name=f"den_ps{t}", tag=f"bank_b{t}") for t in range(PACK)]
+
+        def add_transposed(t, which):
             for b in range(4):
                 blk = slice(b * P, (b + 1) * P)
-                nc.tensor.matmul(den_ps[:, blk], y_sq[t][:, blk], ident[:], start=True, stop=False, is_transpose=True)
-                nc.tensor.matmul(den_ps[:, blk], pa_sq[:, t, blk], ident[:], start=False, stop=True, is_transpose=True)
-            nc.scalar.activation(log_den[:, t, :], den_ps[:], ACT.Ln, bias=quarter[:], scale=0.5)
+                nc.tensor.matmul(
+                    den_ps[t][:, blk], squares[:, which, t, blk], ident[:],
+                    start=(which == 0 and b == 0), stop=(which == 1 and b == 3), is_transpose=True,
+                )
 
         for t in range(PACK):
-            nc.vector.tensor_tensor(st[t][:], y[t][:].indirect(n1_sb[:]), y_copy[t][:], ALU.add)
-            if t == 0:
-                numerator(PACK - 1)
-            else:
-                nc.vector.tensor_scalar(st_gain[t - 1][:], st[t - 1][:], gn_sb[:, t - 1 : t], None, ALU.mult)
-            nc.scalar.activation(tanh_st[t][:], st[t][:], ACT.Tanh)
+            nc.vector.tensor_copy(pa[t][:], y[t][:].indirect(n3_sb[:]))
+            nc.scalar.activation(squares[:, 0, t, :], y[t][:, :S], ACT.Square)
+            add_transposed(t, 0)
+        for t in range(PACK):
+            numerator(t)
+            nc.scalar.activation(squares[:, 1, t, :], pa[t][:], ACT.Square)
+            add_transposed(t, 1)
+        for t in range(PACK):
+            nc.scalar.activation(log_den[:, t, :], den_ps[t][:], ACT.Ln, bias=quarter[:], scale=0.5)
+
+        for t in range(PACK):
+            nc.vector.tensor_tensor(st[t][:], y[t][:].indirect(n1_sb[:]), y_copy[:, t, :], ALU.add)
+            nc.scalar.activation(tanh_st[t][:, :S], st[t][:], ACT.Tanh)
+            nc.scalar.mul(st_gain[t][:], st[t][:], gn_sb[:, t : t + 1])
 
         r_ps = [psum.tile([P, PACK, P], F32, name=f"r_ps{b}", tag=f"bank_b{b}") for b in range(4)]
         for b in range(4):
@@ -185,60 +191,106 @@ def tile_picked_joinhoppharmunder_none_p_kernel(
 
         z = keep.tile([P, PACK, S], F32, name="z", align_bytes=64)
         z_bf = keep.tile([P, PACK * S], BF16, name="z_bf", align_bytes=64)
-        z2_bf = keep.tile([P, PACK * S], BF16, name="z2_bf", align_bytes=64)
-        for half in range(2):
-            for t in range(PACK):
-                nc.vector.tensor_tensor(
-                    z[:, t, cols(half)], tanh_st[t][:].indirect(entries(n2_sb, half)), st_gain[t][:, cols(half)], ALU.mult
-                )
-                if half == 0 and t == 0:
-                    nc.vector.tensor_scalar(st_gain[3][:], st[3][:], gn_sb[:, 3:4], None, ALU.mult)
-            nc.scalar.copy(
-                z_bf[:, half * PACK * HALF : (half + 1) * PACK * HALF].rearrange("p (c i t) -> p c t i", i=4, t=PACK),
-                z[:, :, cols(half)].rearrange("p t (c i) -> p c t i", i=4),
-            )
-
-        w2q, w3q, zq, z2q = (mx_tiles(s) for s in ("w2q", "w3q", "zq", "z2q"))
-        for b in range(4):
+        z2_bf = shared.tile([P, PACK * S], BF16, name="z2_bf", offset=24576 + 4096, align_bytes=64)
+        for t, lo, hi in [(0, 0, S), (1, 0, S), (2, 0, S), (3, 0, HALF), (3, HALF, S)]:
             nc.vector.tensor_tensor(
-                z2_bf[:, b * PACK * P : (b + 1) * PACK * P].rearrange("p (c i t) -> p c t i", i=4, t=PACK),
-                num[:, :, b * P : (b + 1) * P].rearrange("p t (c i) -> p c t i", i=4),
-                r_ps[b][:].rearrange("p t (c i) -> p c t i", i=4),
-                ALU.mult,
+                z[:, t, lo:hi], tanh_st[t][:].indirect(n2_sb[:, lo // 16 : hi // 16]), st_gain[t][:, lo:hi], ALU.mult
             )
-        quantize(w2q, w2_bf, 0, P)
-        quantize(w3q, w3_bf, 0, P)
-
-        h_ps = [psum.tile([P, S], F32, name=f"h_ps{t}", tag=f"bank_a{t}") for t in range(PACK)]
-        h, e4, e5, res = (planes(s) for s in ("h", "e4", "e5", "res"))
-        neg_h = planes("neg_h", 2 * S)
         for half in range(2):
-            quantize(z2q, z2_bf, half * HALF, HALF)
-            quantize(zq, z_bf, half * HALF, HALF)
-        for t in range(1, PACK):
-            quantize(w2q, w2_bf, t * P, P)
-            quantize(w3q, w3_bf, t * P, P)
+            nc.scalar.copy(
+                z_bf[:, half * PACK * HALF : (half + 1) * PACK * HALF].rearrange("p (c i t) -> p c t i", i=2, t=PACK),
+                z[:, :, cols(half)].rearrange("p t (c i) -> p c t i", i=2),
+            )
+
+        zq, z2q = mx_tiles("zq"), mx_tiles("z2q")
+        w_scales = keep.tile([P, 2, 512], U8, name="w_scales", align_bytes=64)
+        first_codes = shared.tile([P, 2, P], U32, name="first_codes", offset=16384, align_bytes=64)
+        later_codes = shared.tile([P, 2, 3 * P], U32, name="later_codes", offset=24576 + 4096, align_bytes=64)
+
+        def weight_mx(which, t, count=1):
+            codes = first_codes[:, which, :] if t == 0 else later_codes[:, which, (t - 1) * P : (t - 1 + count) * P]
+            return codes, w_scales[:, which, t * P : (t + count) * P]
+
+        quantize(weight_mx(0, 0), w2_bf, 0, P)
+        quantize(weight_mx(1, 0), w3_bf, 0, P)
+        for half in range(2):
+            for b in (2 * half, 2 * half + 1):
+                nc.vector.tensor_tensor(
+                    z2_bf[:, b * PACK * P : (b + 1) * PACK * P].rearrange("p (c i t) -> p c t i", i=2, t=PACK),
+                    num[:, :, b * P : (b + 1) * P].rearrange("p t (c i) -> p c t i", i=2),
+                    r_ps[b][:].rearrange("p t (c i) -> p c t i", i=2),
+                    ALU.mult,
+                )
+            quantize(mx_cols(zq, half * HALF, HALF), z_bf, half * HALF, HALF)
+            quantize(mx_cols(z2q, half * HALF, HALF), z2_bf, half * HALF, HALF)
+        for which, w_bf in enumerate((w2_bf, w3_bf)):
+            quantize(weight_mx(which, 1), w_bf, P, P)
+        for which, w_bf in enumerate((w2_bf, w3_bf)):
+            quantize(weight_mx(which, 2, 2), w_bf, 2 * P, 2 * P)
+
+        e4, e5, res = (planes(s) for s in ("e4", "e5", "res"))
+        h, neg_h = planes("h", 2 * S), planes("neg_h", 2 * S)
         for t in range(PACK):
             for half in range(2):
-                product(h_ps[t], w3q, t, z2q, half, True, False)
-                product(h_ps[t], w2q, t, zq, half, False, True)
-                nc.scalar.mul(neg_h[t][:, cols(half)], h_ps[t][:, cols(half)], -1.0)
-                nc.scalar.copy(h[t][:, cols(half)], h_ps[t][:, cols(half)])
+                h_ps = psum.tile([P, HALF], F32, name=f"h_ps{t}{half}", tag=f"bank_{'ab'[half]}{t}")
+                product(h_ps[:], weight_mx(0, t), mx_cols(zq, half * HALF, HALF), True, False)
+                product(h_ps[:], weight_mx(1, t), mx_cols(z2q, half * HALF, HALF), False, True)
+                nc.scalar.mul(neg_h[t][:, cols(half)], h_ps[:], -1.0)
+                nc.scalar.copy(h[t][:, cols(half)], h_ps[:])
 
         out_rows = out.rearrange("(p t) j -> p t j", t=PACK)
-        steps = [(t, 0, S) for t in range(PACK - 1)] + [(PACK - 1, 0, HALF), (PACK - 1, HALF, S)]
 
-        def finish(t, lo, hi):
+        def minus_b(t, lo, hi):
+            nc.vector.tensor_copy(e5[t][:, lo:hi], neg_h[t][:].indirect(n5_sb[:, lo // 16 : hi // 16]))
+
+        def a_minus_b(t, lo, hi):
+            nc.vector.tensor_tensor(
+                e4[t][:, lo:hi], h[t][:].indirect(n4_sb[:, lo // 16 : hi // 16]), e5[t][:, lo:hi], ALU.add
+            )
+
+        def finish_by_sum(t):
+            excess = shared.tile([P, S], F32, name=f"excess{t}", offset=28672 + 2048 * t, align_bytes=64)
+            turned = keep.tile([P, S], F32, name=f"turned{t}", align_bytes=64)
+            nc.scalar.activation(excess[:], e4[t][:], ACT.Relu, scale=-1.0)
+            sum_ps = psum.tile([P, S], F32, name=f"sum_ps{t}", tag=f"bank_{'ba'[t]}3")
+            for term, src in enumerate((h[t], e5[t], excess)):
+                for b in range(4):
+                    blk = slice(b * P, (b + 1) * P)
+                    nc.tensor.matmul(
+                        sum_ps[:, blk], src[:, blk], ident[:],
+                        start=(term == 0 and b == 0), stop=(term == 2 and b == 3), is_transpose=True,
+                    )
+            nc.scalar.copy(turned[:], sum_ps[:])
+            back_ps = psum.tile([P, S], F32, name=f"back_ps{t}", tag=f"bank_b{t}")
+            for b in range(4):
+                blk = slice(b * P, (b + 1) * P)
+                nc.tensor.transpose(back_ps[:, blk], turned[:, blk], ident[:])
+            nc.scalar.copy(res[t][:], back_ps[:])
+            nc.scalar.dma_start(out_rows[:, t, :], res[t][:])
+
+        def h_minus(dst, lst, t, lo, hi):
+            nc.vector.tensor_tensor(
+                dst[t][:, lo:hi], neg_h[t][:].indirect(lst[:, lo // 16 : hi // 16]), h[t][:, lo:hi], ALU.add
+            )
+
+        def finish_by_max(t, lo, hi):
             nc.vector.tensor_tensor(res[t][:, lo:hi], e4[t][:, lo:hi], e5[t][:, lo:hi], ALU.max)
             nc.sync.dma_start(out_rows[:, t, lo:hi], res[t][:, lo:hi])
 
-        for i, (t, lo, hi) in enumerate(steps):
-            nc.vector.tensor_tensor(
-                e4[t][:, lo:hi], neg_h[t][:].indirect(n4_sb[:, lo // 16 : hi // 16]), h[t][:, lo:hi], ALU.add
-            )
-            if i > 0:
-                finish(*steps[i - 1])
-            nc.vector.tensor_tensor(
-                e5[t][:, lo:hi], neg_h[t][:].indirect(n5_sb[:, lo // 16 : hi // 16]), h[t][:, lo:hi], ALU.add
-            )
-        finish(*steps[-1])
+        minus_b(0, 0, HALF)
+        minus_b(0, HALF, S)
+        a_minus_b(0, 0, HALF)
+        a_minus_b(0, HALF, S)
+        minus_b(1, 0, S)
+        h_minus(e4, n4_sb, 2, 0, S)
+        a_minus_b(1, 0, S)
+        finish_by_sum(0)
+        finish_by_sum(1)
+        h_minus(e5, n5_sb, 2, 0, S)
+        h_minus(e4, n4_sb, 3, 0, HALF)
+        finish_by_max(2, 0, S)
+        h_minus(e5, n5_sb, 3, 0, HALF)
+        h_minus(e4, n4_sb, 3, HALF, S)
+        finish_by_max(3, 0, HALF)
+        h_minus(e5, n5_sb, 3, HALF, S)
+        finish_by_max(3, HALF, S)

from contextlib import ExitStack

import concourse.mybir as mybir
from concourse.masks import make_identity

K, T, S, N, H = 512, 2048, 512, 512, 512
FLOPS = 2 * K * H * S + 2 * 2 * H * N * S

F32 = mybir.dt.float32
BF16 = mybir.dt.bfloat16
I32 = mybir.dt.int32
U32 = mybir.dt.uint32
U16 = mybir.dt.uint16
U8 = mybir.dt.uint8
FP8X4 = mybir.dt.float8_e4m3fn_x4
ALU = mybir.AluOpType
ACT = mybir.ActivationFunctionType

P = 128
PACK = 4
HALF = S // 2
LIST_COLS = S // 16


def tile_picked_joinhoppharmunder_none_p_kernel(
    tc, x_words, x_scales, w1, gn, gm, w2, w3, offs, n1, n2, n3, n4, n5, out
):
    nc = tc.nc
    with ExitStack() as ctx:
        keep = ctx.enter_context(tc.tile_pool(name="keep", bufs=1))
        shared = ctx.enter_context(tc.tile_pool(name="shared", bufs=1))
        psum = ctx.enter_context(tc.psum_pool(name="psum", bufs=1))

        def planes(name, width=S):
            return [keep.tile([P, width], F32, name=f"{name}{t}", align_bytes=64) for t in range(PACK)]

        def load_list(name, src):
            tile = keep.tile([P, LIST_COLS], U16, name=name)
            nc.sync.dma_start(tile[:], src)
            return tile

        def load_weight(name, src):
            tile = keep.tile([P, PACK, 512], F32, name=name, align_bytes=64)
            nc.sync.dma_start(tile[:], src.rearrange("(p j) c -> p j c", j=PACK))
            return tile

        def load_gain(name, src):
            tile = keep.tile([P, PACK], F32, name=name)
            nc.sync.dma_start(tile[:], src.rearrange("(p t) o -> p (t o)", t=PACK))
            return tile

        def cols(half):
            return slice(half * HALF, (half + 1) * HALF)

        def entries(lst, half):
            return lst[:, half * LIST_COLS // 2 : (half + 1) * LIST_COLS // 2]

        def deal_views(name, raw, order):
            grouped = keep.tile([P, 4 * 512], BF16, name=name, align_bytes=64)
            dst = grouped[:].rearrange("p (t m j) -> " + order, t=PACK, j=PACK)
            src = raw[:].rearrange("p j (m t) -> " + order, t=PACK)
            return grouped, dst, src

        def mx_tiles(name):
            codes = keep.tile([P, 512], U32, name=name + "_codes", align_bytes=64)
            scales = keep.tile([P, 512], U8, name=name + "_scales", align_bytes=64)
            return codes, scales

        def mx_cols(mx, first, count):
            return mx[0][:, first : first + count], mx[1][:, first : first + count]

        def quantize(mx, grouped, first, count):
            nc.vector.quantize_mx(
                out=mx[0].bitcast(FP8X4), scales=mx[1], in_=grouped[:, PACK * first : PACK * (first + count)]
            )

        def product(acc, lhs, rhs, start, stop):
            nc.tensor.matmul_mx(
                out=acc,
                lhsT=lhs[0].bitcast(FP8X4),
                lhsT_scale=lhs[1],
                rhs=rhs[0].bitcast(FP8X4),
                rhs_scale=rhs[1],
                start=start,
                stop=stop,
            )

        xs_table = keep.tile([P, T], U8, name="xs_table", align_bytes=64)
        xs_rows = keep.tile([P, T], U8, name="xs_rows", align_bytes=64)
        for q in range(4):
            nc.sync.dma_start(
                xs_rows[32 * q : 32 * q + 4, :].bitcast(I32), x_scales[0, 4 * q : 4 * q + 4, :].bitcast(I32)
            )
        nc.vector.memset(xs_table[:].bitcast(I32), 0)
        w1_raw = load_weight("w1_raw", w1)
        offs_sb = load_list("offs_sb", offs)
        xw_table = keep.tile([P, T], U32, name="xw_table", align_bytes=64)
        nc.sync.dma_start(xw_table[:].bitcast(I32), x_words[0].rearrange("p n t -> p (n t)").bitcast(I32))
        n3_sb = load_list("n3_sb", n3)
        gm_sb = load_gain("gm_sb", gm)
        n1_sb = load_list("n1_sb", n1)
        w2_raw = load_weight("w2_raw", w2)
        w3_raw = load_weight("w3_raw", w3)
        gn_sb = load_gain("gn_sb", gn)
        n2_sb = load_list("n2_sb", n2)
        n4_sb = load_list("n4_sb", n4)
        n5_sb = load_list("n5_sb", n5)

        quarter = keep.tile([P, 1], F32, name="quarter")
        nc.gpsimd.memset(quarter[:], 0.25)
        warm = keep.tile([P, 1], F32, name="warm")
        nc.scalar.activation(warm[:], quarter[:], ACT.Ln)
        ident = keep.tile([P, P], F32, name="ident", align_bytes=64)
        make_identity(nc, ident[:])

        xq = mx_tiles("xq")
        for q in range(4):
            rows = slice(32 * q, 32 * q + 4)
            nc.vector.tensor_copy(xs_table[rows, :].bitcast(I32), xs_rows[rows, :].bitcast(I32))
        nc.vector.tensor_copy(xq[1][:], xs_table[:].indirect(offs_sb[:]))
        w1_bf, dst, src = deal_views("w1_bf", w1_raw, "p m t j")
        nc.scalar.copy(dst[:, : P // 2], src[:, : P // 2])
        nc.vector.tensor_copy(dst[:, P // 2 :], src[:, P // 2 :])
        w1q = mx_tiles("w1q")
        for t in range(PACK):
            quantize(mx_cols(w1q, t * P, P), w1_bf, t * P, P)
        y_ps = [psum.tile([P, S], F32, name=f"y_ps{t}", tag=f"bank_a{t}") for t in range(PACK)]
        y = planes("y", 2 * S)
        for half in range(2):
            nc.vector.tensor_copy(xq[0][:, cols(half)], xw_table[:].indirect(entries(offs_sb, half)))
        for t, lo, hi in [(0, 0, HALF), (0, HALF, S), (1, 0, S), (2, 0, S), (3, 0, S)]:
            product(y_ps[t][:, lo:hi], mx_cols(w1q, t * P, P), mx_cols(xq, lo, hi - lo), True, True)
            nc.scalar.copy(y[t][:, lo:hi], y_ps[t][:, lo:hi])

        y_copy = shared.tile([P, PACK, S], F32, name="y_copy", offset=16384, align_bytes=64)
        for t in range(PACK):
            nc.sync.dma_start(y_copy[:, t, :], y[t][:, :S])

        w2_bf, dst, src = deal_views("w2_bf", w2_raw, "p m t j")
        nc.gpsimd.tensor_scalar(dst, src, 1.0, 0.0, ALU.mult, ALU.add)
        w3_bf, dst, src = deal_views("w3_bf", w3_raw, "p m t j")
        nc.gpsimd.tensor_scalar(dst, src, 1.0, 0.0, ALU.mult, ALU.add)

        pa = planes("pa")
        st = [shared.tile([P, S], F32, name=f"st{t}", offset=32768 + t * S * 4, align_bytes=64) for t in range(PACK)]
        st_gain = planes("st_gain")
        squares = shared.tile([P, 2, PACK, S], F32, name="squares", offset=0, align_bytes=64)
        tanh_st = [shared.tile([P, 2 * S], F32, name=f"tanh_st{t}", offset=t * S * 8, align_bytes=64) for t in range(PACK)]
        num = keep.tile([P, PACK, S], F32, name="num", align_bytes=64)
        log_den = keep.tile([P, PACK, S], F32, name="log_den", align_bytes=64)
        recip_t = shared.tile([P, PACK, S], F32, name="recip_t", offset=32768, align_bytes=64)

        def numerator(t):
            nc.vector.scalar_tensor_tensor(
                num[:, t, :], pa[t][:], gm_sb[:, t : t + 1], y_ps[t][:], ALU.mult, ALU.mult
            )

        den_ps = [psum.tile([P, S], F32, name=f"den_ps{t}", tag=f"bank_b{t}") for t in range(PACK)]

        def add_transposed(t, which):
            for b in range(4):
                blk = slice(b * P, (b + 1) * P)
                nc.tensor.matmul(
                    den_ps[t][:, blk], squares[:, which, t, blk], ident[:],
                    start=(which == 0 and b == 0), stop=(which == 1 and b == 3), is_transpose=True,
                )

        for t in range(PACK):
            nc.vector.tensor_copy(pa[t][:], y[t][:].indirect(n3_sb[:]))
            nc.scalar.activation(squares[:, 0, t, :], y[t][:, :S], ACT.Square)
            add_transposed(t, 0)
        for t in range(PACK):
            numerator(t)
            nc.scalar.activation(squares[:, 1, t, :], pa[t][:], ACT.Square)
            add_transposed(t, 1)
        for t in range(PACK):
            nc.scalar.activation(log_den[:, t, :], den_ps[t][:], ACT.Ln, bias=quarter[:], scale=0.5)

        for t in range(PACK):
            nc.vector.tensor_tensor(st[t][:], y[t][:].indirect(n1_sb[:]), y_copy[:, t, :], ALU.add)
            nc.scalar.activation(tanh_st[t][:, :S], st[t][:], ACT.Tanh)
            nc.scalar.mul(st_gain[t][:], st[t][:], gn_sb[:, t : t + 1])

        r_ps = [psum.tile([P, PACK, P], F32, name=f"r_ps{b}", tag=f"bank_b{b}") for b in range(4)]
        for b in range(4):
            blk = slice(b * P, (b + 1) * P)
            nc.scalar.activation(recip_t[:, :, blk], log_den[:, :, blk], ACT.Exp, scale=-1.0)
            for t in range(PACK):
                nc.tensor.transpose(r_ps[b][:, t, :], recip_t[:, t, b * P : (b + 1) * P], ident[:])


        z = keep.tile([P, PACK, S], F32, name="z", align_bytes=64)
        z_bf = keep.tile([P, PACK * S], BF16, name="z_bf", align_bytes=64)
        z2_bf = shared.tile([P, PACK * S], BF16, name="z2_bf", offset=24576 + 4096, align_bytes=64)
        for t, lo, hi in [(0, 0, S), (1, 0, S), (2, 0, S), (3, 0, HALF), (3, HALF, S)]:
            nc.vector.tensor_tensor(
                z[:, t, lo:hi], tanh_st[t][:].indirect(n2_sb[:, lo // 16 : hi // 16]), st_gain[t][:, lo:hi], ALU.mult
            )
        for half in range(2):
            nc.scalar.copy(
                z_bf[:, half * PACK * HALF : (half + 1) * PACK * HALF].rearrange("p (c i t) -> p c t i", i=2, t=PACK),
                z[:, :, cols(half)].rearrange("p t (c i) -> p c t i", i=2),
            )

        zq, z2q = mx_tiles("zq"), mx_tiles("z2q")
        w_scales = keep.tile([P, 2, 512], U8, name="w_scales", align_bytes=64)
        first_codes = shared.tile([P, 2, P], U32, name="first_codes", offset=16384, align_bytes=64)
        later_codes = shared.tile([P, 2, 3 * P], U32, name="later_codes", offset=24576 + 4096, align_bytes=64)

        def weight_mx(which, t, count=1):
            codes = first_codes[:, which, :] if t == 0 else later_codes[:, which, (t - 1) * P : (t - 1 + count) * P]
            return codes, w_scales[:, which, t * P : (t + count) * P]

        quantize(weight_mx(0, 0), w2_bf, 0, P)
        quantize(weight_mx(1, 0), w3_bf, 0, P)
        for half in range(2):
            for b in (2 * half, 2 * half + 1):
                nc.vector.tensor_tensor(
                    z2_bf[:, b * PACK * P : (b + 1) * PACK * P].rearrange("p (c i t) -> p c t i", i=2, t=PACK),
                    num[:, :, b * P : (b + 1) * P].rearrange("p t (c i) -> p c t i", i=2),
                    r_ps[b][:].rearrange("p t (c i) -> p c t i", i=2),
                    ALU.mult,
                )
            quantize(mx_cols(zq, half * HALF, HALF), z_bf, half * HALF, HALF)
            quantize(mx_cols(z2q, half * HALF, HALF), z2_bf, half * HALF, HALF)
        for which, w_bf in enumerate((w2_bf, w3_bf)):
            quantize(weight_mx(which, 1), w_bf, P, P)
        for which, w_bf in enumerate((w2_bf, w3_bf)):
            quantize(weight_mx(which, 2, 2), w_bf, 2 * P, 2 * P)

        e4, e5, res = (planes(s) for s in ("e4", "e5", "res"))
        h, neg_h = planes("h", 2 * S), planes("neg_h", 2 * S)
        for t in range(PACK):
            for half in range(2):
                h_ps = psum.tile([P, HALF], F32, name=f"h_ps{t}{half}", tag=f"bank_{'ab'[half]}{t}")
                product(h_ps[:], weight_mx(0, t), mx_cols(zq, half * HALF, HALF), True, False)
                product(h_ps[:], weight_mx(1, t), mx_cols(z2q, half * HALF, HALF), False, True)
                nc.scalar.mul(neg_h[t][:, cols(half)], h_ps[:], -1.0)
                nc.scalar.copy(h[t][:, cols(half)], h_ps[:])

        out_rows = out.rearrange("(p t) j -> p t j", t=PACK)

        def minus_b(t, lo, hi):
            nc.vector.tensor_copy(e5[t][:, lo:hi], neg_h[t][:].indirect(n5_sb[:, lo // 16 : hi // 16]))

        def a_minus_b(t, lo, hi):
            nc.vector.tensor_tensor(
                e4[t][:, lo:hi], h[t][:].indirect(n4_sb[:, lo // 16 : hi // 16]), e5[t][:, lo:hi], ALU.add
            )

        def finish_by_sum(t):
            excess = shared.tile([P, S], F32, name=f"excess{t}", offset=28672 + 2048 * t, align_bytes=64)
            turned = keep.tile([P, S], F32, name=f"turned{t}", align_bytes=64)
            nc.scalar.activation(excess[:], e4[t][:], ACT.Relu, scale=-1.0)
            sum_ps = psum.tile([P, S], F32, name=f"sum_ps{t}", tag=f"bank_{'ba'[t]}3")
            for term, src in enumerate((h[t], e5[t], excess)):
                for b in range(4):
                    blk = slice(b * P, (b + 1) * P)
                    nc.tensor.matmul(
                        sum_ps[:, blk], src[:, blk], ident[:],
                        start=(term == 0 and b == 0), stop=(term == 2 and b == 3), is_transpose=True,
                    )
            nc.scalar.copy(turned[:], sum_ps[:])
            back_ps = psum.tile([P, S], F32, name=f"back_ps{t}", tag=f"bank_b{t}")
            for b in range(4):
                blk = slice(b * P, (b + 1) * P)
                nc.tensor.transpose(back_ps[:, blk], turned[:, blk], ident[:])
            nc.scalar.copy(res[t][:], back_ps[:])
            nc.scalar.dma_start(out_rows[:, t, :], res[t][:])

        def h_minus(dst, lst, t, lo, hi):
            nc.vector.tensor_tensor(
                dst[t][:, lo:hi], neg_h[t][:].indirect(lst[:, lo // 16 : hi // 16]), h[t][:, lo:hi], ALU.add
            )

        def finish_by_max(t, lo, hi):
            nc.vector.tensor_tensor(res[t][:, lo:hi], e4[t][:, lo:hi], e5[t][:, lo:hi], ALU.max)
            nc.sync.dma_start(out_rows[:, t, lo:hi], res[t][:, lo:hi])

        minus_b(0, 0, HALF)
        minus_b(0, HALF, S)
        a_minus_b(0, 0, HALF)
        a_minus_b(0, HALF, S)
        minus_b(1, 0, S)
        h_minus(e4, n4_sb, 2, 0, S)
        a_minus_b(1, 0, S)
        finish_by_sum(0)
        finish_by_sum(1)
        h_minus(e5, n5_sb, 2, 0, S)
        h_minus(e4, n4_sb, 3, 0, HALF)
        finish_by_max(2, 0, S)
        h_minus(e5, n5_sb, 3, 0, HALF)
        h_minus(e4, n4_sb, 3, HALF, S)
        finish_by_max(3, 0, HALF)
        h_minus(e5, n5_sb, 3, HALF, S)
        finish_by_max(3, HALF, S)
